import numpy as np
import ml_dtypes


def mxq(x, axis, fmt="e4m3"):
    dtype, down = {"e4m3": (ml_dtypes.float8_e4m3fn, 7), "e5m2": (ml_dtypes.float8_e5m2, 14)}[fmt]
    v = np.moveaxis(np.asarray(x, np.float32).astype(ml_dtypes.bfloat16).astype(np.float64), axis, -1)
    blocks = v.reshape(v.shape[:-1] + (-1, 32))
    amax = np.abs(blocks).max(-1, keepdims=True)
    byte = np.maximum(np.where(amax > 0, np.frexp(amax)[1] - 1 + 127, 0) - down, 1)
    scale = np.exp2(byte - 127.0)
    codes = (blocks / scale).astype(np.float32).astype(dtype).astype(np.float64)
    return np.moveaxis((codes * scale).reshape(v.shape), -1, axis)


WIDE = False


def mx_kscale(k):
    if not WIDE:
        return np.ones(k)
    levels = np.array([24, -24, 12, -12, 0])
    if k % 512:
        return np.exp2(np.random.permutation(np.resize(levels, k // 32))).repeat(32)
    a = np.empty((k // 512, 16))
    for p in range(k // 512):
        a[p, :8] = np.random.permutation(np.resize(levels, 8))
        for g in range(8):
            far = levels[np.abs(levels - a[p, g]) >= 10]
            a[p, g + 8] = far[np.random.randint(len(far))]
    return np.exp2(a.ravel()).repeat(32)


def f64(x):
    return np.asarray(x).astype(np.float64)


def striped(idx):
    return np.tile(idx.reshape(-1, 16).T, (8, 1)).astype(np.uint16)


def unstriped(offs):
    return offs[:16].T.reshape(-1).astype(np.int64)


E2M1 = np.array([0.0, 0.5, 1.0, 1.5, 2.0, 3.0, 4.0, 6.0, -0.0, -0.5, -1.0, -1.5, -2.0, -3.0, -4.0, -6.0])


def pack_weight(w, fmt):
    k, n = w.shape
    w = f64(np.asarray(w, np.float32).astype(ml_dtypes.bfloat16)).reshape(k // 32, 32, n)
    amax = np.abs(w).max(1)
    if fmt == "e4m3":
        byte = np.frexp(amax)[1] - 1 + 127 - 7
    else:
        mant, ex = np.frexp(amax / 6.0)
        byte = np.where(mant > 0.5, ex, ex - 1) + 127
    byte = np.clip(np.where(amax > 0, byte, 1), 1, 254)
    scaled = (w * np.exp2(127.0 - byte)[:, None, :]).reshape(k, n).astype(np.float32)
    by_word = np.ascontiguousarray(scaled.reshape(k // 512, 128, 4, n).transpose(0, 1, 3, 2))
    if fmt == "e4m3":
        words = by_word.astype(ml_dtypes.float8_e4m3fn).view(np.uint8)
    else:
        c = by_word.astype(ml_dtypes.float4_e2m1fn).view(np.uint8) & 0xF
        words = (c[..., 0::2] | (c[..., 1::2] << 4)).reshape(k // 512, 128, 2 * n)
    return np.ascontiguousarray(words), np.ascontiguousarray(byte.astype(np.uint8).reshape(k // 512, 16, n))


def unpack_weight(words, scales, fmt):
    g, _, n = scales.shape
    words = np.ascontiguousarray(words).reshape(g, 128, n, -1)
    if fmt == "e4m3":
        vals = words.view(ml_dtypes.float8_e4m3fn).astype(np.float64)
    else:
        nib = np.empty((g, 128, n, 4), np.uint8)
        nib[..., 0::2] = words & 0xF
        nib[..., 1::2] = words >> 4
        vals = E2M1[nib]
    vals = vals * np.repeat(np.exp2(scales.astype(np.float64) - 127.0), 8, axis=1)[..., None]
    return vals.transpose(0, 1, 3, 2).reshape(g * 512, n)


def gelu(f):
    return 0.5 * f * (1.0 + np.tanh(np.sqrt(2.0 / np.pi) * (f + 0.044715 * f**3)))


K, R, N, T, J = 512, 1024, 512, 2048, 1024


def setup_inputs():
    n = np.random.standard_normal
    s = mx_kscale(K)[:, None]
    u = mx_kscale(R)[:, None]
    p_tab = pack_weight(n((K, T)) * s, "e4m3")
    p_w1 = pack_weight(n((K, R)) / np.sqrt(3 * K) / s * u.T, "e2m1")
    p_w2 = pack_weight(n((K, R)) / np.sqrt(3 * K) / s * u.T, "e2m1")
    return {
        "tab_words": p_tab[0],
        "tab_scales": p_tab[1],
        "w0": (n((K, R)) / np.sqrt(3 * K) / s * u.T).astype(np.float32),
        "w1_words": p_w1[0],
        "w1_scales": p_w1[1],
        "w2_words": p_w2[0],
        "w2_scales": p_w2[1],
        "wd": (n((R, N)) / np.sqrt(R) / u).astype(np.float32),
        "b": (0.3 * n(N)).astype(np.float32),
        "offs": striped(np.concatenate([np.random.permutation(T)[:J] for _ in range(3)])),
    }


def reference(tab_words, tab_scales, w0, w1_words, w1_scales, w2_words, w2_scales, wd, b, offs):
    idx = unstriped(offs).reshape(3, J)
    tab_ = unpack_weight(tab_words, tab_scales, "e4m3")[:, idx]
    w0_ = mxq(f64(w0), 0, "e4m3")
    w1_ = unpack_weight(w1_words, w1_scales, "e2m1")
    w2_ = unpack_weight(w2_words, w2_scales, "e2m1")
    a = w0_.T @ tab_[:, 0] + w1_.T @ tab_[:, 1] + w2_.T @ tab_[:, 2]
    h = np.maximum(a, 0.0)
    h_ = mxq(h, 0, "e4m3")
    wd_ = mxq(f64(wd), 0, "e4m3")
    y = wd_.T @ h_
    return gelu(y + f64(b)[:, None])

@@ -1,0 +1,201 @@
+from contextlib import ExitStack
+
+import concourse.mybir as mybir
+
+K, R, N, T, J = 512, 1024, 512, 2048, 1024
+FLOPS = 2 * J * (3 * K * R + R * N)
+
+F32 = mybir.dt.float32
+BF16 = mybir.dt.bfloat16
+I32 = mybir.dt.int32
+U32 = mybir.dt.uint32
+U16 = mybir.dt.uint16
+U8 = mybir.dt.uint8
+E4M3 = mybir.dt.float8_e4m3fn_x4
+E2M1 = mybir.dt.float4_e2m1fn_x4
+ACT = mybir.ActivationFunctionType
+
+P = 128
+PACK = 4
+PASS = P * PACK
+CHUNK = 256
+CHUNKS = J // CHUNK
+GROUP = 128
+
+
+def tile_list_rvq_relu_gelu_kernel(
+    tc, tab_words, tab_scales, w0, w1_words, w1_scales, w2_words, w2_scales, wd, b, offs, out
+):
+    nc = tc.nc
+    with ExitStack() as ctx:
+        keep = ctx.enter_context(tc.tile_pool(name="keep", bufs=1))
+        stage = ctx.enter_context(tc.tile_pool(name="stage", bufs=2))
+        ring = ctx.enter_context(tc.tile_pool(name="ring", bufs=1))
+        reuse = ctx.enter_context(tc.tile_pool(name="reuse", bufs=1))
+        acc_pool = ctx.enter_context(tc.psum_pool(name="acc_pool", bufs=5))
+        y_pool = ctx.enter_context(tc.psum_pool(name="y_pool", bufs=3))
+
+        def tile(shape, dtype, name):
+            return keep.tile(shape, dtype, name=name, align_bytes=64)
+
+        offsets = keep.tile([P, 3 * J // 16], U16, name="offsets")
+        table = tile([P, T], I32, "table")
+        table_planes = tile([P, T // 4], I32, "table_planes")
+        fp4_planes_raw = reuse.tile([P, 2 * R // 4], I32, name="reuse_planes", align_bytes=64)
+        fp4_words = tile([P, 2 * R * 2], U8, "fp4_words")
+        fp4_planes = tile([P, 2 * R], U8, "fp4_planes")
+        bias = tile([P, PACK], F32, "bias")
+        warm = tile([P, 2], F32, "warm")
+
+        nc.gpsimd.memset(warm[:, 0:1], 0.0)
+        nc.scalar.activation(warm[:, 1:2], warm[:, 0:1], ACT.Gelu_apprx_tanh)
+        nc.vector.memset(table_planes[:], 0)
+        nc.vector.memset(fp4_planes_raw[:], 0)
+
+        def staged(shape, dtype):
+            return stage.tile(shape, dtype, name="staged", align_bytes=64)
+
+        def load_planes(dst, src):
+            rows = src[0].bitcast(I32)
+            for q in range(4):
+                nc.scalar.dma_start(out=dst[32 * q : 32 * q + 4, :], in_=rows[4 * q : 4 * q + 4, :])
+
+        nc.sync.dma_start(offsets[:], offs)
+        fp4_raw = [staged([P, R // 2], I32) for w in range(2)]
+        nc.sync.dma_start(out=fp4_raw[0][:], in_=w1_words[0].bitcast(I32))
+        nc.sync.dma_start(out=fp4_raw[1][:], in_=w2_words[0].bitcast(I32))
+        nc.sync.dma_start(out=table[:], in_=tab_words[0].rearrange("p t i -> p (t i)").bitcast(I32))
+        load_planes(table_planes, tab_scales)
+        load_planes(fp4_planes_raw[:, 0 : R // 4], w1_scales)
+        load_planes(fp4_planes_raw[:, R // 4 : R // 2], w2_scales)
+        nc.gpsimd.dma_start(out=bias[:], in_=b.rearrange("(p t) -> p t", t=PACK))
+
+        for w in range(2):
+            nc.vector.tensor_copy(
+                out=fp4_words[:, 2 * R * w : 2 * R * (w + 1)].bitcast(U16).rearrange("p (h t m) -> p h t m", t=PACK, m=P),
+                in_=fp4_raw[w][:].bitcast(U16).rearrange("p (h m t) -> p h t m", t=PACK, m=P),
+            )
+
+        w0_rows = w0.rearrange("(p i) r -> p i r", i=PACK)
+        w0_raw = [staged([P, 2, PACK, 256], F32), staged([P, PACK, PASS], F32)]
+        nc.sync.dma_start(out=w0_raw[0][:, 0], in_=w0_rows[:, :, 0:256])
+        nc.sync.dma_start(out=w0_raw[0][:, 1], in_=w0_rows[:, :, 256:512])
+        nc.sync.dma_start(out=w0_raw[1][:], in_=w0_rows[:, :, 512:1024])
+        wd_rows = wd.rearrange("(h p i) n -> h p i n", h=2, i=PACK)
+
+        def round_and_interleave(copy, grouped, raw, m0, m1, raw_m0):
+            dst = grouped[:].rearrange("p (u t m i) -> p u m i t", u=2, t=2, i=PACK)
+            src = raw.rearrange("p i (m u t) -> p u m i t", u=2, t=2)
+            for u in range(2):
+                copy(out=dst[:, u, m0:m1], in_=src[:, u, raw_m0 : raw_m0 + m1 - m0])
+
+        def quantize(grouped, name):
+            width = grouped.shape[1] // PACK
+            codes = tile([P, width], U32, name + "_codes")
+            planes = tile([P, width], U8, name + "_planes")
+            nc.vector.quantize_mx(out=codes[:].bitcast(E4M3), scales=planes[:], in_=grouped[:])
+            return codes, planes
+
+        def gather(c):
+            if c % 2 == 1:
+                words = reuse.tile([P, 3, CHUNK], U32, name="reuse_words", align_bytes=64)
+                planes = reuse.tile([P, 3, CHUNK], U8, name="reuse_planes", align_bytes=64)
+            else:
+                words = ring.tile([P, 3, CHUNK], U32, name="picked_words%d" % (c % 2), align_bytes=64)
+                planes = ring.tile([P, 3, CHUNK], U8, name="picked_planes%d" % (c % 2), align_bytes=64)
+            for g in (1, 2, 0):
+                col = (g * J + c * CHUNK) // 16
+                piece = offsets[:, col : col + CHUNK // 16]
+                nc.vector.tensor_copy(words[:, g, :], table[:].bitcast(U32).indirect(piece))
+                nc.vector.tensor_copy(planes[:, g, :], table_planes[:].bitcast(U8).indirect(piece))
+            return words, planes
+
+        picked = {0: gather(0)}
+
+        w0_q = []
+        planes_dst = fp4_planes[:].rearrange("p (w h t m) -> p h w t m", w=2, t=PACK, m=P)
+        planes_src = fp4_planes_raw[:].bitcast(U8).rearrange("p (w h m t) -> p h w t m", w=2, t=PACK, m=P)
+        for h in range(2):
+            if h == 0:
+                grouped = reuse.tile([P, PASS * PACK], BF16, name="reuse_words", align_bytes=64)
+                round_and_interleave(nc.scalar.copy, grouped, w0_raw[0][:, 0], 0, 64, 0)
+                round_and_interleave(nc.scalar.copy, grouped, w0_raw[0][:, 1], 64, 128, 0)
+            else:
+                grouped = tile([P, PASS * PACK], BF16, "w0_grouped1")
+                round_and_interleave(nc.scalar.copy, grouped, w0_raw[1][:], 0, 128, 0)
+            nc.vector.tensor_copy(out=planes_dst[:, h], in_=planes_src[:, h])
+            w0_q.append(quantize(grouped, "w0_%d" % h))
+
+        wd_raw = [staged([P, PACK, N], F32) for h in range(2)]
+        for h in range(2):
+            nc.sync.dma_start(out=wd_raw[h][:], in_=wd_rows[h])
+
+        def first_layer(c, h):
+            words, planes = picked[c]
+            grouped = tile([P, CHUNK * PACK], BF16, "h_grouped%d_%d" % (c, h))
+            for s in range(CHUNK // GROUP):
+                cols = slice(s * GROUP, (s + 1) * GROUP)
+                acc = acc_pool.tile([P, PACK, GROUP], F32, name="acc")
+                for t in range(PACK):
+                    col = h * PASS + t * P
+                    for g in (1, 2, 0):
+                        if g == 0:
+                            lhsT = w0_q[h][0][:, t * P : (t + 1) * P].bitcast(E4M3)
+                            lhsT_scale = w0_q[h][1][:, t * P : (t + 1) * P]
+                        else:
+                            first = (g - 1) * R + col
+                            lhsT = fp4_words[:, 2 * first : 2 * (first + P)].bitcast(E2M1)
+                            lhsT_scale = fp4_planes[:, first : first + P]
+                        nc.tensor.matmul_mx(
+                            out=acc[:, t, :],
+                            lhsT=lhsT,
+                            lhsT_scale=lhsT_scale,
+                            rhs=words[:, g, cols].bitcast(E4M3),
+                            rhs_scale=planes[:, g, cols],
+                            start=(g == 1),
+                            stop=(g == 0),
+                        )
+                nc.scalar.activation(
+                    grouped[:, s * GROUP * PACK : (s + 1) * GROUP * PACK].rearrange("p (j t) -> p j t", t=PACK),
+                    acc[:].rearrange("p t j -> p j t"),
+                    ACT.Relu,
+                )
+            return quantize(grouped, "h%d_%d" % (c, h))
+
+        out_rows = out.rearrange("(p t) j -> p t j", t=PACK)
+
+        def second_layer(c, h_q, wd_q):
+            for u in range(2):
+                y = y_pool.tile([P, 2, CHUNK], F32, name="y")
+                result = tile([P, 2, CHUNK], F32, "result%d_%d" % (c, u))
+                for e in range(2):
+                    t = 2 * u + e
+                    for h in range(2):
+                        nc.tensor.matmul_mx(
+                            out=y[:, e, :],
+                            lhsT=wd_q[h][0][:, t * P : (t + 1) * P].bitcast(E4M3),
+                            lhsT_scale=wd_q[h][1][:, t * P : (t + 1) * P],
+                            rhs=h_q[h][0][:].bitcast(E4M3),
+                            rhs_scale=h_q[h][1][:],
+                            start=(h == 0),
+                            stop=(h == 1),
+                        )
+                for e in range(2):
+                    t = 2 * u + e
+                    nc.scalar.activation(result[:, e, :], y[:, e, :], ACT.Gelu_apprx_tanh, bias=bias[:, t : t + 1])
+                nc.sync.dma_start(out=out_rows[:, 2 * u : 2 * u + 2, c * CHUNK : (c + 1) * CHUNK], in_=result[:])
+
+        h_q = {}
+        wd_q = []
+        for c in range(CHUNKS):
+            h_q[c] = [first_layer(c, h) for h in range(2)]
+            if c + 1 < CHUNKS:
+                picked[c + 1] = gather(c + 1)
+            if c == 1:
+                for h in range(2):
+                    grouped = tile([P, PASS * PACK], BF16, "wd_grouped%d" % h)
+                    round_and_interleave(nc.scalar.copy, grouped, wd_raw[h][:], 0, 128, 0)
+                    wd_q.append(quantize(grouped, "wd_%d" % h))
+            if c >= 1:
+                second_layer(c - 1, h_q[c - 1], wd_q)
+        second_layer(CHUNKS - 1, h_q[CHUNKS - 1], wd_q)

@@ -23,179 +23,198 @@ CHUNKS = J // CHUNK
 GROUP = 128
 
 
+CFG = {'text': [('C0', 0), ('G', 0, 'w'), ('CD', 0), ('G', 0, 'p'), ('G', 1, 'w'), ('CD', 1), ('CD', 2), ('C0', 1), ('G', 1, 'p'), ('PS', 0), ('C0', 2), ('C0', 3), ('Q0', 0), ('PW', 0), ('QD', 0), ('F', 0, 0, 0), ('F', 0, 0, 1), ('PW', 1), ('CD', 3), ('PS', 1), ('G', 2, 'w'), ('Q0', 1), ('F', 1, 0, 0), ('HQ', 0, 0), ('QD', 1), ('F', 1, 0, 1), ('G', 3, 'w'), ('G', 2, 'p'), ('F', 0, 1, 0), ('F', 0, 1, 1), ('F', 1, 1, 0), ('F', 1, 1, 1), ('G', 3, 'p'), ('F', 2, 0, 0), ('F', 2, 0, 1), ('HQ', 1, 0), ('HQ', 0, 1), ('F', 2, 1, 0), ('S', 0, 0), ('HQ', 1, 1), ('S', 0, 1), ('F', 2, 1, 1), ('F', 3, 0, 0), ('F', 3, 0, 1), ('S', 1, 0), ('F', 3, 1, 0), ('HQ', 2, 0), ('F', 3, 1, 1), ('S', 1, 1), ('HQ', 2, 1), ('S', 2, 0), ('S', 2, 1), ('HQ', 3, 0), ('HQ', 3, 1), ('S', 3, 0), ('S', 3, 1)], 'dma': ['w1w', 'tabs', 'offs', 'w01', 'w2s', 'w2w', 'w00', 'w1s', 'tab', 'w03', 'w02', 'wd0', 'wd1', 'bias'], 'eng': {'r301': 'V', 'r010': 'V', 'r300': 'V'}, 'reuse': {'pw3': 'wdg1', 'hg11': 'wdr1', 'hg20': 'wdr1', 'hg21': 'wdr1', 'pp2': 'w0r2', 'pp3': 'wdg0', 'hg01': 'wdr0', 'hg10': 'wdr1', 'hg00': 'w0r3'}, 'banks': {'a': [0, 1, 2, 3, 4, 5, 6, 7], 'y': []}, 'sharebanks': True, 'w2sq': 'SP'}
+
+
 def tile_list_rvq_relu_gelu_kernel(
     tc, tab_words, tab_scales, w0, w1_words, w1_scales, w2_words, w2_scales, wd, b, offs, out
 ):
     nc = tc.nc
+    reuse = CFG["reuse"]
+    eng = CFG["eng"]
     with ExitStack() as ctx:
         keep = ctx.enter_context(tc.tile_pool(name="keep", bufs=1))
-        stage = ctx.enter_context(tc.tile_pool(name="stage", bufs=2))
-        ring = ctx.enter_context(tc.tile_pool(name="ring", bufs=1))
-        reuse = ctx.enter_context(tc.tile_pool(name="reuse", bufs=1))
-        acc_pool = ctx.enter_context(tc.psum_pool(name="acc_pool", bufs=5))
-        y_pool = ctx.enter_context(tc.psum_pool(name="y_pool", bufs=3))
+        psum = ctx.enter_context(tc.psum_pool(name="psum", bufs=1))
+        made = {}
+
+        def tag_of(name):
+            while name in reuse:
+                name = reuse[name]
+            return name
 
         def tile(shape, dtype, name):
-            return keep.tile(shape, dtype, name=name, align_bytes=64)
+            if name not in made:
+                if name in reuse:
+                    group = [k for k in reuse if reuse[k] == reuse[name]]
+                    whole = keep.tile([P, len(group)] + shape[1:], dtype, name=tag_of(name), align_bytes=64)
+                    for n, k in enumerate(group):
+                        made[k] = whole[:, n]
+                else:
+                    made[name] = keep.tile(shape, dtype, name=name, align_bytes=64)[:]
+            return made[name]
+
+        count = {"a": 0, "y": 0}
+
+        def bank(kind, shape):
+            if CFG["sharebanks"]:
+                kind = "a"
+            names = CFG["banks"][kind]
+            k = names[count[kind] % len(names)]
+            count[kind] = count[kind] + 1
+            return psum.tile(shape, F32, name="bank%d" % k)
 
         offsets = keep.tile([P, 3 * J // 16], U16, name="offsets")
         table = tile([P, T], I32, "table")
         table_planes = tile([P, T // 4], I32, "table_planes")
-        fp4_planes_raw = reuse.tile([P, 2 * R // 4], I32, name="reuse_planes", align_bytes=64)
-        fp4_words = tile([P, 2 * R * 2], U8, "fp4_words")
-        fp4_planes = tile([P, 2 * R], U8, "fp4_planes")
+        fp4_planes_raw = tile([P, R // 2], I32, "plr")
+        fp4_raw = tile([P, R], I32, "f4r")
+        fp4_words = tile([P, R], I32, "fp4_words")
+        fp4_planes = tile([P, R // 2], I32, "fp4_planes")
         bias = tile([P, PACK], F32, "bias")
         warm = tile([P, 2], F32, "warm")
 
         nc.gpsimd.memset(warm[:, 0:1], 0.0)
         nc.scalar.activation(warm[:, 1:2], warm[:, 0:1], ACT.Gelu_apprx_tanh)
-        nc.vector.memset(table_planes[:], 0)
-        nc.vector.memset(fp4_planes_raw[:], 0)
+        nc.vector.memset(table_planes, 0)
+        nc.vector.memset(fp4_planes_raw, 0)
 
-        def staged(shape, dtype):
-            return stage.tile(shape, dtype, name="staged", align_bytes=64)
-
-        def load_planes(dst, src):
+        def load_planes(queue, dst, src):
             rows = src[0].bitcast(I32)
             for q in range(4):
-                nc.scalar.dma_start(out=dst[32 * q : 32 * q + 4, :], in_=rows[4 * q : 4 * q + 4, :])
-
-        nc.sync.dma_start(offsets[:], offs)
-        fp4_raw = [staged([P, R // 2], I32) for w in range(2)]
-        nc.sync.dma_start(out=fp4_raw[0][:], in_=w1_words[0].bitcast(I32))
-        nc.sync.dma_start(out=fp4_raw[1][:], in_=w2_words[0].bitcast(I32))
-        nc.sync.dma_start(out=table[:], in_=tab_words[0].rearrange("p t i -> p (t i)").bitcast(I32))
-        load_planes(table_planes, tab_scales)
-        load_planes(fp4_planes_raw[:, 0 : R // 4], w1_scales)
-        load_planes(fp4_planes_raw[:, R // 4 : R // 2], w2_scales)
-        nc.gpsimd.dma_start(out=bias[:], in_=b.rearrange("(p t) -> p t", t=PACK))
-
-        for w in range(2):
-            nc.vector.tensor_copy(
-                out=fp4_words[:, 2 * R * w : 2 * R * (w + 1)].bitcast(U16).rearrange("p (h t m) -> p h t m", t=PACK, m=P),
-                in_=fp4_raw[w][:].bitcast(U16).rearrange("p (h m t) -> p h t m", t=PACK, m=P),
-            )
+                queue.dma_start(out=dst[32 * q : 32 * q + 4, :], in_=rows[4 * q : 4 * q + 4, :])
 
         w0_rows = w0.rearrange("(p i) r -> p i r", i=PACK)
-        w0_raw = [staged([P, 2, PACK, 256], F32), staged([P, PACK, PASS], F32)]
-        nc.sync.dma_start(out=w0_raw[0][:, 0], in_=w0_rows[:, :, 0:256])
-        nc.sync.dma_start(out=w0_raw[0][:, 1], in_=w0_rows[:, :, 256:512])
-        nc.sync.dma_start(out=w0_raw[1][:], in_=w0_rows[:, :, 512:1024])
-        wd_rows = wd.rearrange("(h p i) n -> h p i n", h=2, i=PACK)
+        wd_rows = wd.rearrange("(h s t e) n -> h e s t n", h=2, t=PACK, e=4)
+        for nm in CFG["dma"]:
+            if nm == "offs":
+                nc.sync.dma_start(offsets[:], offs)
+            elif nm == "tab":
+                nc.sync.dma_start(out=table, in_=tab_words[0].rearrange("p t i -> p (t i)").bitcast(I32))
+            elif nm == "tabs":
+                load_planes(nc.sync, table_planes, tab_scales)
+            elif nm == "w1s":
+                load_planes(nc.sync, fp4_planes_raw[:, 0 : R // 4], w1_scales)
+            elif nm == "w2s":
+                load_planes(nc.gpsimd if CFG.get("w2sq", "G") == "G" else nc.sync, fp4_planes_raw[:, R // 4 : R // 2], w2_scales)
+            elif nm in ("w1w", "w2w"):
+                w = int(nm[1]) - 1
+                nc.sync.dma_start(out=fp4_raw[:, 512 * w : 512 * (w + 1)], in_=(w1_words, w2_words)[w][0].bitcast(I32))
+            elif nm in ("w1a", "w2a", "w1b", "w2b"):
+                w = int(nm[1]) - 1
+                h = "ab".index(nm[2])
+                nc.sync.dma_start(out=fp4_raw[:, 512 * w + 256 * h : 512 * w + 256 * (h + 1)], in_=(w1_words, w2_words)[w][0].bitcast(I32)[:, 256 * h : 256 * (h + 1)])
+            elif nm.startswith("w0"):
+                k = int(nm[2])
+                nc.sync.dma_start(out=tile([P, PACK, 256], F32, "w0r%d" % k), in_=w0_rows[:, :, 256 * k : 256 * (k + 1)])
+            elif nm.startswith("wd"):
+                h = int(nm[2])
+                raw = tile([P, PACK, N], F32, "wdr%d" % h)
+                for e in range(4):
+                    nc.sync.dma_start(out=raw[e:P:4], in_=wd_rows[h, e])
+            else:
+                with nc.allow_non_contiguous_dma(reason="one bias value a partition"):
+                    nc.sync.dma_start(out=bias, in_=b.rearrange("(t p) -> p t", t=PACK))
 
-        def round_and_interleave(copy, grouped, raw, m0, m1, raw_m0):
-            dst = grouped[:].rearrange("p (u t m i) -> p u m i t", u=2, t=2, i=PACK)
-            src = raw.rearrange("p i (m u t) -> p u m i t", u=2, t=2)
-            for u in range(2):
-                copy(out=dst[:, u, m0:m1], in_=src[:, u, raw_m0 : raw_m0 + m1 - m0])
+        def cast(nm, dst, src):
+            e = eng.get(nm, "A")
+            if e == "A":
+                nc.scalar.copy(out=dst, in_=src)
+            elif e == "V":
+                nc.vector.tensor_copy(out=dst, in_=src)
+            else:
+                nc.gpsimd.tensor_copy(out=dst, in_=src)
 
         def quantize(grouped, name):
             width = grouped.shape[1] // PACK
             codes = tile([P, width], U32, name + "_codes")
             planes = tile([P, width], U8, name + "_planes")
-            nc.vector.quantize_mx(out=codes[:].bitcast(E4M3), scales=planes[:], in_=grouped[:])
+            nc.vector.quantize_mx(out=codes.bitcast(E4M3), scales=planes, in_=grouped)
             return codes, planes
 
-        def gather(c):
-            if c % 2 == 1:
-                words = reuse.tile([P, 3, CHUNK], U32, name="reuse_words", align_bytes=64)
-                planes = reuse.tile([P, 3, CHUNK], U8, name="reuse_planes", align_bytes=64)
-            else:
-                words = ring.tile([P, 3, CHUNK], U32, name="picked_words%d" % (c % 2), align_bytes=64)
-                planes = ring.tile([P, 3, CHUNK], U8, name="picked_planes%d" % (c % 2), align_bytes=64)
-            for g in (1, 2, 0):
-                col = (g * J + c * CHUNK) // 16
-                piece = offsets[:, col : col + CHUNK // 16]
-                nc.vector.tensor_copy(words[:, g, :], table[:].bitcast(U32).indirect(piece))
-                nc.vector.tensor_copy(planes[:, g, :], table_planes[:].bitcast(U8).indirect(piece))
-            return words, planes
-
-        picked = {0: gather(0)}
-
-        w0_q = []
-        planes_dst = fp4_planes[:].rearrange("p (w h t m) -> p h w t m", w=2, t=PACK, m=P)
-        planes_src = fp4_planes_raw[:].bitcast(U8).rearrange("p (w h m t) -> p h w t m", w=2, t=PACK, m=P)
-        for h in range(2):
-            if h == 0:
-                grouped = reuse.tile([P, PASS * PACK], BF16, name="reuse_words", align_bytes=64)
-                round_and_interleave(nc.scalar.copy, grouped, w0_raw[0][:, 0], 0, 64, 0)
-                round_and_interleave(nc.scalar.copy, grouped, w0_raw[0][:, 1], 64, 128, 0)
-            else:
-                grouped = tile([P, PASS * PACK], BF16, "w0_grouped1")
-                round_and_interleave(nc.scalar.copy, grouped, w0_raw[1][:], 0, 128, 0)
-            nc.vector.tensor_copy(out=planes_dst[:, h], in_=planes_src[:, h])
-            w0_q.append(quantize(grouped, "w0_%d" % h))
-
-        wd_raw = [staged([P, PACK, N], F32) for h in range(2)]
-        for h in range(2):
-            nc.sync.dma_start(out=wd_raw[h][:], in_=wd_rows[h])
-
-        def first_layer(c, h):
-            words, planes = picked[c]
-            grouped = tile([P, CHUNK * PACK], BF16, "h_grouped%d_%d" % (c, h))
-            for s in range(CHUNK // GROUP):
+        words_dst = fp4_words.rearrange("p (w h t s e) -> p h w t s e", w=2, h=2, t=PACK, e=2)
+        words_src = fp4_raw.rearrange("p (w h s t e) -> p h w t s e", w=2, h=2, t=PACK, e=2)
+        planes_dst = fp4_planes.rearrange("p (w h t s) -> p h w t s", w=2, h=2, t=PACK)
+        planes_src = fp4_planes_raw.rearrange("p (w h s t) -> p h w t s", w=2, h=2, t=PACK)
+        out_rows = out.rearrange("(t p) j -> p t j", t=PACK)
+        q = {}
+        for step in CFG["text"]:
+            k = step[0]
+            if k == "G":
+                c = step[1]
+                for g in (1, 2, 0):
+                    col = (g * J + c * CHUNK) // 16
+                    piece = offsets[:, col : col + CHUNK // 16]
+                    if step[2] == "w":
+                        nc.vector.tensor_copy(tile([P, 3, CHUNK], U32, "pw%d" % c)[:, g, :], table.bitcast(U32).indirect(piece))
+                    else:
+                        nc.vector.tensor_copy(tile([P, 3, CHUNK], U8, "pp%d" % c)[:, g, :], table_planes.bitcast(U8).indirect(piece))
+            elif k == "C0":
+                n = step[1]
+                grouped = tile([P, PASS * PACK], BF16, "w0g%d" % (n // 2))
+                dst = grouped.rearrange("p (t s e i) -> p t s i e", t=PACK, e=4, i=PACK)
+                src = made["w0r%d" % n].rearrange("p i (s t e) -> p t s i e", t=PACK, e=4)
+                cast("c0%d" % n, dst[:, :, 16 * (n % 2) : 16 * (n % 2) + 16], src)
+            elif k == "Q0":
+                q["w0", step[1]] = quantize(made["w0g%d" % step[1]], "w0q%d" % step[1])
+            elif k == "PW":
+                nc.vector.tensor_copy(out=words_dst[:, step[1]], in_=words_src[:, step[1]])
+            elif k == "PS":
+                nc.vector.tensor_copy(out=planes_dst[:, step[1]], in_=planes_src[:, step[1]])
+            elif k == "CD":
+                n = step[1]
+                grouped = tile([P, PASS * PACK], BF16, "wdg%d" % (n // 2))
+                dst = grouped.rearrange("p (c e t) -> p c t e", e=4, t=PACK)
+                src = made["wdr%d" % (n // 2)].rearrange("p t (c e) -> p c t e", e=4)
+                cols = slice(64 * (n % 2), 64 * (n % 2) + 64)
+                cast("cd%d" % n, dst[:, cols], src[:, cols])
+            elif k == "QD":
+                q["wd", step[1]] = quantize(made["wdg%d" % step[1]], "wdq%d" % step[1])
+            elif k == "F":
+                c, h, s = step[1:]
+                words = made["pw%d" % c]
+                planes = made["pp%d" % c]
                 cols = slice(s * GROUP, (s + 1) * GROUP)
-                acc = acc_pool.tile([P, PACK, GROUP], F32, name="acc")
+                acc = bank("a", [P, PACK, GROUP])
                 for t in range(PACK):
-                    col = h * PASS + t * P
                     for g in (1, 2, 0):
                         if g == 0:
-                            lhsT = w0_q[h][0][:, t * P : (t + 1) * P].bitcast(E4M3)
-                            lhsT_scale = w0_q[h][1][:, t * P : (t + 1) * P]
+                            lhsT = q["w0", h][0][:, t * P : (t + 1) * P].bitcast(E4M3)
+                            lhsT_scale = q["w0", h][1][:, t * P : (t + 1) * P]
                         else:
-                            first = (g - 1) * R + col
-                            lhsT = fp4_words[:, 2 * first : 2 * (first + P)].bitcast(E2M1)
-                            lhsT_scale = fp4_planes[:, first : first + P]
+                            first = (g - 1) * R + h * PASS + t * P
+                            lhsT = fp4_words[:, first // 2 : (first + P) // 2].bitcast(E2M1)
+                            lhsT_scale = fp4_planes[:, first // 4 : (first + P) // 4].bitcast(U8)
                         nc.tensor.matmul_mx(
-                            out=acc[:, t, :],
-                            lhsT=lhsT,
-                            lhsT_scale=lhsT_scale,
-                            rhs=words[:, g, cols].bitcast(E4M3),
-                            rhs_scale=planes[:, g, cols],
-                            start=(g == 1),
-                            stop=(g == 0),
+                            out=acc[:, t, :], lhsT=lhsT, lhsT_scale=lhsT_scale, rhs=words[:, g, cols].bitcast(E4M3),
+                            rhs_scale=planes[:, g, cols], start=(g == 1), stop=(g == 0),
                         )
-                nc.scalar.activation(
-                    grouped[:, s * GROUP * PACK : (s + 1) * GROUP * PACK].rearrange("p (j t) -> p j t", t=PACK),
-                    acc[:].rearrange("p t j -> p j t"),
-                    ACT.Relu,
-                )
-            return quantize(grouped, "h%d_%d" % (c, h))
-
-        out_rows = out.rearrange("(p t) j -> p t j", t=PACK)
-
-        def second_layer(c, h_q, wd_q):
-            for u in range(2):
-                y = y_pool.tile([P, 2, CHUNK], F32, name="y")
-                result = tile([P, 2, CHUNK], F32, "result%d_%d" % (c, u))
-                for e in range(2):
-                    t = 2 * u + e
+                grouped = tile([P, CHUNK * PACK], BF16, "hg%d%d" % (c, h))
+                dst = grouped[:, s * GROUP * PACK : (s + 1) * GROUP * PACK].rearrange("p (j t) -> p j t", t=PACK)
+                if eng.get("r%d%d%d" % (c, h, s), "A") == "A":
+                    nc.scalar.activation(dst, acc[:].rearrange("p t j -> p j t"), ACT.Relu)
+                else:
+                    nc.vector.tensor_scalar_max(dst, acc[:].rearrange("p t j -> p j t"), 0.0)
+            elif k == "HQ":
+                c, h = step[1:]
+                q["h", c, h] = quantize(made["hg%d%d" % (c, h)], "hq%d%d" % (c, h))
+            elif k == "HQ1":
+                c, h, s = step[1:]
+                q["h", c, h, s] = quantize(made["hg%d%d" % (c, h)][:, s * 512 : (s + 1) * 512], "hq%d%d%d" % (c, h, s))
+            else:
+                c, u = step[1:]
+                ts = [2 * u, 2 * u + 1] if k == "S" else [0, 1, 2, 3]
+                width = CHUNK if k == "S" else GROUP
+                j0 = c * CHUNK + (0 if k == "S" else u * GROUP)
+                y = bank("y", [P, len(ts), width])
+                for e, t in enumerate(ts):
                     for h in range(2):
+                        hq = q["h", c, h] if k == "S" else q["h", c, h, u]
                         nc.tensor.matmul_mx(
-                            out=y[:, e, :],
-                            lhsT=wd_q[h][0][:, t * P : (t + 1) * P].bitcast(E4M3),
-                            lhsT_scale=wd_q[h][1][:, t * P : (t + 1) * P],
-                            rhs=h_q[h][0][:].bitcast(E4M3),
-                            rhs_scale=h_q[h][1][:],
-                            start=(h == 0),
-                            stop=(h == 1),
+                            out=y[:, e, :], lhsT=q["wd", h][0][:, t * P : (t + 1) * P].bitcast(E4M3),
+                            lhsT_scale=q["wd", h][1][:, t * P : (t + 1) * P], rhs=hq[0].bitcast(E4M3), rhs_scale=hq[1],
+                            start=(h == 0), stop=(h == 1),
                         )
-                for e in range(2):
-                    t = 2 * u + e
+                result = tile([P, 512], F32, "res%d%d" % (c, u)).rearrange("p (e j) -> p e j", e=len(ts))
+                for e, t in enumerate(ts):
                     nc.scalar.activation(result[:, e, :], y[:, e, :], ACT.Gelu_apprx_tanh, bias=bias[:, t : t + 1])
-                nc.sync.dma_start(out=out_rows[:, 2 * u : 2 * u + 2, c * CHUNK : (c + 1) * CHUNK], in_=result[:])
-
-        h_q = {}
-        wd_q = []
-        for c in range(CHUNKS):
-            h_q[c] = [first_layer(c, h) for h in range(2)]
-            if c + 1 < CHUNKS:
-                picked[c + 1] = gather(c + 1)
-            if c == 1:
-                for h in range(2):
-                    grouped = tile([P, PASS * PACK], BF16, "wd_grouped%d" % h)
-                    round_and_interleave(nc.scalar.copy, grouped, wd_raw[h][:], 0, 128, 0)
-                    wd_q.append(quantize(grouped, "wd_%d" % h))
-            if c >= 1:
-                second_layer(c - 1, h_q[c - 1], wd_q)
-        second_layer(CHUNKS - 1, h_q[CHUNKS - 1], wd_q)
+                nc.sync.dma_start(out=out_rows[:, ts[0] : ts[-1] + 1, j0 : j0 + width], in_=result)

@@ -23,7 +23,7 @@ CHUNKS = J // CHUNK
 GROUP = 128
 
 
-CFG = {'text': [('C0', 0), ('G', 0, 'w'), ('CD', 0), ('G', 0, 'p'), ('G', 1, 'w'), ('CD', 1), ('CD', 2), ('C0', 1), ('G', 1, 'p'), ('PS', 0), ('C0', 2), ('C0', 3), ('Q0', 0), ('PW', 0), ('QD', 0), ('F', 0, 0, 0), ('F', 0, 0, 1), ('PW', 1), ('CD', 3), ('PS', 1), ('G', 2, 'w'), ('Q0', 1), ('F', 1, 0, 0), ('HQ', 0, 0), ('QD', 1), ('F', 1, 0, 1), ('G', 3, 'w'), ('G', 2, 'p'), ('F', 0, 1, 0), ('F', 0, 1, 1), ('F', 1, 1, 0), ('F', 1, 1, 1), ('G', 3, 'p'), ('F', 2, 0, 0), ('F', 2, 0, 1), ('HQ', 1, 0), ('HQ', 0, 1), ('F', 2, 1, 0), ('S', 0, 0), ('HQ', 1, 1), ('S', 0, 1), ('F', 2, 1, 1), ('F', 3, 0, 0), ('F', 3, 0, 1), ('S', 1, 0), ('F', 3, 1, 0), ('HQ', 2, 0), ('F', 3, 1, 1), ('S', 1, 1), ('HQ', 2, 1), ('S', 2, 0), ('S', 2, 1), ('HQ', 3, 0), ('HQ', 3, 1), ('S', 3, 0), ('S', 3, 1)], 'dma': ['w1w', 'tabs', 'offs', 'w01', 'w2s', 'w2w', 'w00', 'w1s', 'tab', 'w03', 'w02', 'wd0', 'wd1', 'bias'], 'eng': {'r301': 'V', 'r010': 'V', 'r300': 'V'}, 'reuse': {'pw3': 'wdg1', 'hg11': 'wdr1', 'hg20': 'wdr1', 'hg21': 'wdr1', 'pp2': 'w0r2', 'pp3': 'wdg0', 'hg01': 'wdr0', 'hg10': 'wdr1', 'hg00': 'w0r3'}, 'banks': {'a': [0, 1, 2, 3, 4, 5, 6, 7], 'y': []}, 'sharebanks': True, 'w2sq': 'SP'}
+CFG = {'text': [('C0', 0), ('G', 0, 'w'), ('CD', 0), ('C0', 1), ('CD', 1), ('PW', 0), ('CD', 2), ('PS', 0), ('QD', 0), ('CD', 3), ('G', 1, 'w'), ('G', 0, 'p'), ('C0', 2), ('Q0', 0), ('G', 2, 'w'), ('F', 0, 0), ('F', 1, 0), ('QD', 1), ('C0', 3), ('PW', 1), ('Q0', 1), ('F', 2, 0), ('F', 3, 0), ('F', 0, 1), ('F', 1, 1), ('G', 3, 'w'), ('F', 2, 1), ('G', 1, 'p'), ('HQ', 0, 1), ('HQ', 1, 1), ('F', 3, 1), ('HQ', 0, 0), ('F', 4, 0), ('F', 5, 0), ('S', 0, 0), ('F', 4, 1), ('HQ', 2, 1), ('S', 0, 1), ('F', 5, 1), ('F', 6, 0), ('HQ', 1, 0), ('S', 1, 0), ('F', 7, 0), ('F', 6, 1), ('S', 1, 1), ('F', 7, 1), ('HQ', 3, 0), ('HQ', 2, 0), ('S', 2, 0), ('S', 2, 1), ('HQ', 3, 1), ('S', 3, 0), ('S', 3, 1)], 'dma': ['w2a', 'offs', 'w1a', 'tabs', 'w01', 'w2s', 'w00', 'w1s', 'tab', 'w03', 'w2b', 'w02', 'w1b', 'wd0', 'bias', 'wd1'], 'eng': {'r01': 'V', 'r71': 'V', 'r70': 'V', 'r60': 'V', 'r41': 'V'}, 'reuse': {'pw3': 'wdg1', 'hg11': 'wdr1', 'hg20': 'wdr1', 'hg21': 'wdr1', 'pp1': 'w0r2', 'hg01': 'wdr0', 'hg10': 'wdr1', 'hg00': 'wdr0'}, 'banks': {'a': [0, 1, 2, 3, 4, 5, 6, 7], 'y': []}, 'sharebanks': True, 'w2sq': 'SP', 'gw': [(0, 1), (2, 3), (4, 5), (6, 7)], 'gp': [(0, 1, 2, 3), (4, 5, 6, 7)], 's2': [(0, 1), (2, 3), (4, 5), (6, 7)], 'onep': False, 'pair': True}
 
 
 def tile_list_rvq_relu_gelu_kernel(
@@ -76,11 +76,15 @@ def tile_list_rvq_relu_gelu_kernel(
         nc.gpsimd.memset(warm[:, 0:1], 0.0)
         nc.scalar.activation(warm[:, 1:2], warm[:, 0:1], ACT.Gelu_apprx_tanh)
         nc.vector.memset(table_planes, 0)
-        nc.vector.memset(fp4_planes_raw, 0)
+        if CFG["w2sq"] == "G":
+            nc.vector.memset(fp4_planes_raw[:, 0 : R // 4], 0)
+            nc.gpsimd.memset(fp4_planes_raw[:, R // 4 : R // 2], 0)
+        else:
+            nc.vector.memset(fp4_planes_raw, 0)
 
         def load_planes(queue, dst, src):
             rows = src[0].bitcast(I32)
-            for q in range(4):
+            for q in (0, 2, 1, 3):
                 queue.dma_start(out=dst[32 * q : 32 * q + 4, :], in_=rows[4 * q : 4 * q + 4, :])
 
         w0_rows = w0.rearrange("(p i) r -> p i r", i=PACK)
@@ -102,7 +106,7 @@ def tile_list_rvq_relu_gelu_kernel(
             elif nm in ("w1a", "w2a", "w1b", "w2b"):
                 w = int(nm[1]) - 1
                 h = "ab".index(nm[2])
-                nc.sync.dma_start(out=fp4_raw[:, 512 * w + 256 * h : 512 * w + 256 * (h + 1)], in_=(w1_words, w2_words)[w][0].bitcast(I32)[:, 256 * h : 256 * (h + 1)])
+                nc.sync.dma_start(out=fp4_raw[:, 512 * h + 256 * w : 512 * h + 256 * (w + 1)], in_=(w1_words, w2_words)[w][0].bitcast(I32)[:, 256 * h : 256 * (h + 1)])
             elif nm.startswith("w0"):
                 k = int(nm[2])
                 nc.sync.dma_start(out=tile([P, PACK, 256], F32, "w0r%d" % k), in_=w0_rows[:, :, 256 * k : 256 * (k + 1)])
@@ -131,23 +135,28 @@ def tile_list_rvq_relu_gelu_kernel(
             nc.vector.quantize_mx(out=codes.bitcast(E4M3), scales=planes, in_=grouped)
             return codes, planes
 
-        words_dst = fp4_words.rearrange("p (w h t s e) -> p h w t s e", w=2, h=2, t=PACK, e=2)
-        words_src = fp4_raw.rearrange("p (w h s t e) -> p h w t s e", w=2, h=2, t=PACK, e=2)
+        words_dst = fp4_words.rearrange("p (h w t s e) -> p h w t s e", w=2, h=2, t=PACK, e=2)
+        words_src = fp4_raw.rearrange("p (h w s t e) -> p h w t s e", w=2, h=2, t=PACK, e=2)
         planes_dst = fp4_planes.rearrange("p (w h t s) -> p h w t s", w=2, h=2, t=PACK)
         planes_src = fp4_planes_raw.rearrange("p (w h s t) -> p h w t s", w=2, h=2, t=PACK)
         out_rows = out.rearrange("(t p) j -> p t j", t=PACK)
         q = {}
+        gw = {j: i for i, g in enumerate(CFG["gw"]) for j in g}
+        gp = {j: i for i, g in enumerate(CFG["gp"]) for j in g}
+        s2 = {j: i for i, g in enumerate(CFG["s2"]) for j in g}
         for step in CFG["text"]:
             k = step[0]
             if k == "G":
-                c = step[1]
+                i = step[1]
+                blocks = CFG["g" + step[2]][i]
+                width = GROUP * len(blocks)
                 for g in (1, 2, 0):
-                    col = (g * J + c * CHUNK) // 16
-                    piece = offsets[:, col : col + CHUNK // 16]
+                    col = (g * J + blocks[0] * GROUP) // 16
+                    piece = offsets[:, col : col + width // 16]
                     if step[2] == "w":
-                        nc.vector.tensor_copy(tile([P, 3, CHUNK], U32, "pw%d" % c)[:, g, :], table.bitcast(U32).indirect(piece))
+                        nc.vector.tensor_copy(tile([P, 3, width], U32, "pw%d" % i)[:, g, :], table.bitcast(U32).indirect(piece))
                     else:
-                        nc.vector.tensor_copy(tile([P, 3, CHUNK], U8, "pp%d" % c)[:, g, :], table_planes.bitcast(U8).indirect(piece))
+                        nc.vector.tensor_copy(tile([P, 3, width], U8, "pp%d" % i)[:, g, :], table_planes.bitcast(U8).indirect(piece))
             elif k == "C0":
                 n = step[1]
                 grouped = tile([P, PASS * PACK], BF16, "w0g%d" % (n // 2))
@@ -157,9 +166,18 @@ def tile_list_rvq_relu_gelu_kernel(
             elif k == "Q0":
                 q["w0", step[1]] = quantize(made["w0g%d" % step[1]], "w0q%d" % step[1])
             elif k == "PW":
-                nc.vector.tensor_copy(out=words_dst[:, step[1]], in_=words_src[:, step[1]])
+                if not CFG["onep"]:
+                    nc.vector.tensor_copy(out=words_dst[:, step[1]], in_=words_src[:, step[1]])
+                elif step[1] == 0:
+                    nc.vector.tensor_copy(
+                        out=fp4_words.rearrange("p (w t s e) -> p w t s e", w=4, t=PACK, e=2),
+                        in_=fp4_raw.rearrange("p (w s t e) -> p w t s e", w=4, t=PACK, e=2),
+                    )
             elif k == "PS":
-                nc.vector.tensor_copy(out=planes_dst[:, step[1]], in_=planes_src[:, step[1]])
+                nc.vector.tensor_copy(
+                    out=fp4_planes.rearrange("p (w t s) -> p w t s", w=4, t=PACK),
+                    in_=fp4_planes_raw.rearrange("p (w s t) -> p w t s", w=4, t=PACK),
+                )
             elif k == "CD":
                 n = step[1]
                 grouped = tile([P, PASS * PACK], BF16, "wdg%d" % (n // 2))
@@ -170,11 +188,12 @@ def tile_list_rvq_relu_gelu_kernel(
             elif k == "QD":
                 q["wd", step[1]] = quantize(made["wdg%d" % step[1]], "wdq%d" % step[1])
             elif k == "F":
-                c, h, s = step[1:]
-                words = made["pw%d" % c]
-                planes = made["pp%d" % c]
-                cols = slice(s * GROUP, (s + 1) * GROUP)
-                acc = bank("a", [P, PACK, GROUP])
+                j0, h = step[1:]
+                if CFG.get("pair"):
+                    js = [] if j0 % 2 else [j0, j0 + 1]
+                else:
+                    js = [j0]
+                accs = [bank("a", [P, PACK, GROUP]) for j in js]
                 for t in range(PACK):
                     for g in (1, 2, 0):
                         if g == 0:
@@ -182,39 +201,46 @@ def tile_list_rvq_relu_gelu_kernel(
                             lhsT_scale = q["w0", h][1][:, t * P : (t + 1) * P]
                         else:
                             first = (g - 1) * R + h * PASS + t * P
-                            lhsT = fp4_words[:, first // 2 : (first + P) // 2].bitcast(E2M1)
+                            word = (h * R + (g - 1) * PASS + t * P) // 2
+                            lhsT = fp4_words[:, word : word + P // 2].bitcast(E2M1)
                             lhsT_scale = fp4_planes[:, first // 4 : (first + P) // 4].bitcast(U8)
-                        nc.tensor.matmul_mx(
-                            out=acc[:, t, :], lhsT=lhsT, lhsT_scale=lhsT_scale, rhs=words[:, g, cols].bitcast(E4M3),
-                            rhs_scale=planes[:, g, cols], start=(g == 1), stop=(g == 0),
-                        )
-                grouped = tile([P, CHUNK * PACK], BF16, "hg%d%d" % (c, h))
-                dst = grouped[:, s * GROUP * PACK : (s + 1) * GROUP * PACK].rearrange("p (j t) -> p j t", t=PACK)
-                if eng.get("r%d%d%d" % (c, h, s), "A") == "A":
-                    nc.scalar.activation(dst, acc[:].rearrange("p t j -> p j t"), ACT.Relu)
-                else:
-                    nc.vector.tensor_scalar_max(dst, acc[:].rearrange("p t j -> p j t"), 0.0)
+                        for j, acc in zip(js, accs):
+                            cw = (j - CFG["gw"][gw[j]][0]) * GROUP
+                            cp = (j - CFG["gp"][gp[j]][0]) * GROUP
+                            nc.tensor.matmul_mx(
+                                out=acc[:, t, :], lhsT=lhsT, lhsT_scale=lhsT_scale,
+                                rhs=made["pw%d" % gw[j]][:, g, cw : cw + GROUP].bitcast(E4M3),
+                                rhs_scale=made["pp%d" % gp[j]][:, g, cp : cp + GROUP], start=(g == 1), stop=(g == 0),
+                            )
+                for j, acc in zip(js, accs):
+                    blocks = CFG["s2"][s2[j]]
+                    grouped = tile([P, len(blocks) * GROUP * PACK], BF16, "hg%d%d" % (s2[j], h))
+                    s = j - blocks[0]
+                    dst = grouped[:, s * GROUP * PACK : (s + 1) * GROUP * PACK].rearrange("p (j t) -> p j t", t=PACK)
+                    if eng.get("r%d%d" % (j, h), "A") == "A":
+                        nc.scalar.activation(dst, acc[:].rearrange("p t j -> p j t"), ACT.Relu)
+                    else:
+                        nc.vector.tensor_scalar_max(dst, acc[:].rearrange("p t j -> p j t"), 0.0)
             elif k == "HQ":
-                c, h = step[1:]
-                q["h", c, h] = quantize(made["hg%d%d" % (c, h)], "hq%d%d" % (c, h))
-            elif k == "HQ1":
-                c, h, s = step[1:]
-                q["h", c, h, s] = quantize(made["hg%d%d" % (c, h)][:, s * 512 : (s + 1) * 512], "hq%d%d%d" % (c, h, s))
+                i, h = step[1:]
+                q["h", i, h] = quantize(made["hg%d%d" % (i, h)], "hq%d%d" % (i, h))
             else:
-                c, u = step[1:]
-                ts = [2 * u, 2 * u + 1] if k == "S" else [0, 1, 2, 3]
-                width = CHUNK if k == "S" else GROUP
-                j0 = c * CHUNK + (0 if k == "S" else u * GROUP)
-                y = bank("y", [P, len(ts), width])
+                i, u = step[1:]
+                blocks = CFG["s2"][i]
+                per = PACK // len(blocks)
+                ts = list(range(u * per, (u + 1) * per))
+                width = GROUP * len(blocks)
+                j0 = blocks[0] * GROUP
+                y = bank("y", [P, per, width])
                 for e, t in enumerate(ts):
                     for h in range(2):
-                        hq = q["h", c, h] if k == "S" else q["h", c, h, u]
+                        hq = q["h", i, h]
                         nc.tensor.matmul_mx(
                             out=y[:, e, :], lhsT=q["wd", h][0][:, t * P : (t + 1) * P].bitcast(E4M3),
                             lhsT_scale=q["wd", h][1][:, t * P : (t + 1) * P], rhs=hq[0].bitcast(E4M3), rhs_scale=hq[1],
                             start=(h == 0), stop=(h == 1),
                         )
-                result = tile([P, 512], F32, "res%d%d" % (c, u)).rearrange("p (e j) -> p e j", e=len(ts))
+                result = tile([P, 512], F32, "res%d%d" % (i, u)).rearrange("p (e j) -> p e j", e=per)
                 for e, t in enumerate(ts):
                     nc.scalar.activation(result[:, e, :], y[:, e, :], ACT.Gelu_apprx_tanh, bias=bias[:, t : t + 1])
                 nc.sync.dma_start(out=out_rows[:, ts[0] : ts[-1] + 1, j0 : j0 + width], in_=result)

@@ -23,7 +23,7 @@ CHUNKS = J // CHUNK
 GROUP = 128
 
 
-CFG = {'text': [('C0', 0), ('G', 0, 'w'), ('CD', 0), ('C0', 1), ('CD', 1), ('PW', 0), ('CD', 2), ('PS', 0), ('QD', 0), ('CD', 3), ('G', 1, 'w'), ('G', 0, 'p'), ('C0', 2), ('Q0', 0), ('G', 2, 'w'), ('F', 0, 0), ('F', 1, 0), ('QD', 1), ('C0', 3), ('PW', 1), ('Q0', 1), ('F', 2, 0), ('F', 3, 0), ('F', 0, 1), ('F', 1, 1), ('G', 3, 'w'), ('F', 2, 1), ('G', 1, 'p'), ('HQ', 0, 1), ('HQ', 1, 1), ('F', 3, 1), ('HQ', 0, 0), ('F', 4, 0), ('F', 5, 0), ('S', 0, 0), ('F', 4, 1), ('HQ', 2, 1), ('S', 0, 1), ('F', 5, 1), ('F', 6, 0), ('HQ', 1, 0), ('S', 1, 0), ('F', 7, 0), ('F', 6, 1), ('S', 1, 1), ('F', 7, 1), ('HQ', 3, 0), ('HQ', 2, 0), ('S', 2, 0), ('S', 2, 1), ('HQ', 3, 1), ('S', 3, 0), ('S', 3, 1)], 'dma': ['w2a', 'offs', 'w1a', 'tabs', 'w01', 'w2s', 'w00', 'w1s', 'tab', 'w03', 'w2b', 'w02', 'w1b', 'wd0', 'bias', 'wd1'], 'eng': {'r01': 'V', 'r71': 'V', 'r70': 'V', 'r60': 'V', 'r41': 'V'}, 'reuse': {'pw3': 'wdg1', 'hg11': 'wdr1', 'hg20': 'wdr1', 'hg21': 'wdr1', 'pp1': 'w0r2', 'hg01': 'wdr0', 'hg10': 'wdr1', 'hg00': 'wdr0'}, 'banks': {'a': [0, 1, 2, 3, 4, 5, 6, 7], 'y': []}, 'sharebanks': True, 'w2sq': 'SP', 'gw': [(0, 1), (2, 3), (4, 5), (6, 7)], 'gp': [(0, 1, 2, 3), (4, 5, 6, 7)], 's2': [(0, 1), (2, 3), (4, 5), (6, 7)], 'onep': False, 'pair': True}
+CFG = {'text': [('G', 0, 'w'), ('G', 0, 'p'), ('C0', 0), ('C0', 1), ('PW', 0), ('PS', 0), ('Q0', 0), ('G', 1, 'w'), ('C0', 2), ('C0', 3), ('Q0', 1), ('PW', 1), ('W', 4), ('F', 0, 0), ('F', 1, 0), ('F', 2, 0), ('F', 3, 0), ('G', 2, 'w'), ('G', 1, 'p'), ('G', 3, 'w'), ('G', 2, 'p'), ('HQ', 0, 0), ('CD', 0), ('CD', 1), ('QD', 0), ('CD', 2), ('CD', 3), ('QD', 1), ('F', 0, 1), ('F', 1, 1), ('F', 2, 1), ('F', 3, 1), ('HQ', 0, 1), ('F', 4, 0), ('F', 5, 0), ('F', 4, 1), ('F', 5, 1), ('F', 6, 0), ('F', 7, 0), ('HQ', 1, 0), ('F', 6, 1), ('F', 7, 1), ('HQ', 1, 1), ('S', 0, 0), ('S', 0, 1), ('S', 0, 2), ('S', 0, 3), ('S', 1, 0), ('S', 1, 1), ('S', 1, 2), ('S', 1, 3)], 'dma': ['w1a', 'offs', 'w2a', 'tabs', 'w2s', 'w00', 'w1s', 'w01', 'tab', 'w02', 'w03', 'w2b', 'w1b', 'wd0', 'wd1', 'bias'], 'eng': {'r61': 'V', 'cd1': 'V', 'r70': 'V'}, 'reuse': {'pw2': 'w0g1', 'pw3': 'w0g1', 'pp1': 'f4r', 'pp2': 'f4r', 'hg00': 'w0r3', 'hg01': 'wdr1', 'hg10': 'wdr1', 'hg11': 'wdr1'}, 'banks': {'a': [0, 1, 2, 3, 4, 5, 6, 7], 'y': []}, 'sharebanks': True, 'w2sq': 'G', 'gw': [(0, 1), (2, 3), (4, 5), (6, 7)], 'gp': [(0, 1, 2, 3), (4, 5), (6, 7)], 's2': [(0, 1, 2, 3), (4, 5, 6, 7)], 'onep': False, 'pair': True, 'fine': False}
 
 
 def tile_list_rvq_relu_gelu_kernel(
@@ -221,6 +221,14 @@ def tile_list_rvq_relu_gelu_kernel(
                         nc.scalar.activation(dst, acc[:].rearrange("p t j -> p j t"), ACT.Relu)
                     else:
                         nc.vector.tensor_scalar_max(dst, acc[:].rearrange("p t j -> p j t"), 0.0)
+            elif k == "W":
+                idle = psum.tile([P, 2, 256], F32, name="bank7")
+                for e in range(step[1]):
+                    nc.tensor.matmul_mx(
+                        out=idle[:, e % 2, :], lhsT=fp4_words[:, 64 * (e % 4) : 64 * (e % 4) + 64].bitcast(E2M1),
+                        lhsT_scale=fp4_planes[:, 32 * (e % 4) : 32 * (e % 4) + 32].bitcast(U8),
+                        rhs=made["pw0"][:, 1, 0:256].bitcast(E4M3), rhs_scale=made["pp0"][:, 1, 0:256], start=True, stop=True,
+                    )
             elif k == "HQ":
                 i, h = step[1:]
                 q["h", i, h] = quantize(made["hg%d%d" % (i, h)], "hq%d%d" % (i, h))

@@ -18,237 +18,223 @@ ACT = mybir.ActivationFunctionType
 P = 128
 PACK = 4
 PASS = P * PACK
+RUN = 4
+LIST_GROUP = 16
+BANK_J = 128
 CHUNK = 256
-CHUNKS = J // CHUNK
-GROUP = 128
-
-
-CFG = {'text': [('G', 0, 'w'), ('G', 0, 'p'), ('C0', 0), ('C0', 1), ('PW', 0), ('PS', 0), ('Q0', 0), ('G', 1, 'w'), ('C0', 2), ('C0', 3), ('Q0', 1), ('PW', 1), ('W', 4), ('F', 0, 0), ('F', 1, 0), ('F', 2, 0), ('F', 3, 0), ('G', 2, 'w'), ('G', 1, 'p'), ('G', 3, 'w'), ('G', 2, 'p'), ('HQ', 0, 0), ('CD', 0), ('CD', 1), ('QD', 0), ('CD', 2), ('CD', 3), ('QD', 1), ('F', 0, 1), ('F', 1, 1), ('F', 2, 1), ('F', 3, 1), ('HQ', 0, 1), ('F', 4, 0), ('F', 5, 0), ('F', 4, 1), ('F', 5, 1), ('F', 6, 0), ('F', 7, 0), ('HQ', 1, 0), ('F', 6, 1), ('F', 7, 1), ('HQ', 1, 1), ('S', 0, 0), ('S', 0, 1), ('S', 0, 2), ('S', 0, 3), ('S', 1, 0), ('S', 1, 1), ('S', 1, 2), ('S', 1, 3)], 'dma': ['w1a', 'offs', 'w2a', 'tabs', 'w2s', 'w00', 'w1s', 'w01', 'tab', 'w02', 'w03', 'w2b', 'w1b', 'wd0', 'wd1', 'bias'], 'eng': {'r61': 'V', 'cd1': 'V', 'r70': 'V'}, 'reuse': {'pw2': 'w0g1', 'pw3': 'w0g1', 'pp1': 'f4r', 'pp2': 'f4r', 'hg00': 'w0r3', 'hg01': 'wdr1', 'hg10': 'wdr1', 'hg11': 'wdr1'}, 'banks': {'a': [0, 1, 2, 3, 4, 5, 6, 7], 'y': []}, 'sharebanks': True, 'w2sq': 'G', 'gw': [(0, 1), (2, 3), (4, 5), (6, 7)], 'gp': [(0, 1, 2, 3), (4, 5), (6, 7)], 's2': [(0, 1, 2, 3), (4, 5, 6, 7)], 'onep': False, 'pair': True, 'fine': False}
+WIDE = 512
+W0_PIECE = 256
+WD_PIECE = 256
+BANKS = 8
+LIST_ORDER = (1, 2, 0)
+RELU_ON_VECTOR = ((7, 0), (7, 1))
 
 
 def tile_list_rvq_relu_gelu_kernel(
     tc, tab_words, tab_scales, w0, w1_words, w1_scales, w2_words, w2_scales, wd, b, offs, out
 ):
     nc = tc.nc
-    reuse = CFG["reuse"]
-    eng = CFG["eng"]
     with ExitStack() as ctx:
-        keep = ctx.enter_context(tc.tile_pool(name="keep", bufs=1))
+        sbuf = ctx.enter_context(tc.tile_pool(name="sbuf", bufs=1))
         psum = ctx.enter_context(tc.psum_pool(name="psum", bufs=1))
-        made = {}
-
-        def tag_of(name):
-            while name in reuse:
-                name = reuse[name]
-            return name
 
         def tile(shape, dtype, name):
-            if name not in made:
-                if name in reuse:
-                    group = [k for k in reuse if reuse[k] == reuse[name]]
-                    whole = keep.tile([P, len(group)] + shape[1:], dtype, name=tag_of(name), align_bytes=64)
-                    for n, k in enumerate(group):
-                        made[k] = whole[:, n]
-                else:
-                    made[name] = keep.tile(shape, dtype, name=name, align_bytes=64)[:]
-            return made[name]
+            return sbuf.tile(shape, dtype, name=name, align_bytes=64)[:]
 
-        count = {"a": 0, "y": 0}
+        banks_taken = []
 
-        def bank(kind, shape):
-            if CFG["sharebanks"]:
-                kind = "a"
-            names = CFG["banks"][kind]
-            k = names[count[kind] % len(names)]
-            count[kind] = count[kind] + 1
-            return psum.tile(shape, F32, name="bank%d" % k)
+        def next_bank(shape):
+            banks_taken.append(shape)
+            return psum.tile(shape, F32, name="bank%d" % ((len(banks_taken) - 1) % BANKS))[:]
 
-        offsets = keep.tile([P, 3 * J // 16], U16, name="offsets")
-        table = tile([P, T], I32, "table")
-        table_planes = tile([P, T // 4], I32, "table_planes")
-        fp4_planes_raw = tile([P, R // 2], I32, "plr")
-        fp4_raw = tile([P, R], I32, "f4r")
-        fp4_words = tile([P, R], I32, "fp4_words")
-        fp4_planes = tile([P, R // 2], I32, "fp4_planes")
-        bias = tile([P, PACK], F32, "bias")
+        offsets = sbuf.tile([P, 3 * J // LIST_GROUP], U16, name="offsets")
+        table_words = tile([P, T], I32, "table_words")
+        table_scales = tile([P, T // 4], I32, "table_scales")
+        fp4_scales_raw = tile([P, 2, R // 4], I32, "fp4_scales_raw")
+        fp4_words_raw = tile([P, 2, 2, PASS // 2], I32, "fp4_words_raw")
+        fp4_words = tile([P, 2, 2, PASS // 2], I32, "fp4_words")
+        fp4_scales = tile([P, 2, 2, PASS // 4], I32, "fp4_scales")
+        bias = tile([P, N // P], F32, "bias")
         warm = tile([P, 2], F32, "warm")
 
         nc.gpsimd.memset(warm[:, 0:1], 0.0)
         nc.scalar.activation(warm[:, 1:2], warm[:, 0:1], ACT.Gelu_apprx_tanh)
-        nc.vector.memset(table_planes, 0)
-        if CFG["w2sq"] == "G":
-            nc.vector.memset(fp4_planes_raw[:, 0 : R // 4], 0)
-            nc.gpsimd.memset(fp4_planes_raw[:, R // 4 : R // 2], 0)
-        else:
-            nc.vector.memset(fp4_planes_raw, 0)
 
-        def load_planes(queue, dst, src):
-            rows = src[0].bitcast(I32)
-            for q in (0, 2, 1, 3):
-                queue.dma_start(out=dst[32 * q : 32 * q + 4, :], in_=rows[4 * q : 4 * q + 4, :])
+        nc.vector.memset(table_scales, 0)
+        nc.vector.memset(fp4_scales_raw.rearrange("p w c -> p (w c)"), 0)
 
-        w0_rows = w0.rearrange("(p i) r -> p i r", i=PACK)
-        wd_rows = wd.rearrange("(h s t e) n -> h e s t n", h=2, t=PACK, e=4)
-        for nm in CFG["dma"]:
-            if nm == "offs":
-                nc.sync.dma_start(offsets[:], offs)
-            elif nm == "tab":
-                nc.sync.dma_start(out=table, in_=tab_words[0].rearrange("p t i -> p (t i)").bitcast(I32))
-            elif nm == "tabs":
-                load_planes(nc.sync, table_planes, tab_scales)
-            elif nm == "w1s":
-                load_planes(nc.sync, fp4_planes_raw[:, 0 : R // 4], w1_scales)
-            elif nm == "w2s":
-                load_planes(nc.gpsimd if CFG.get("w2sq", "G") == "G" else nc.sync, fp4_planes_raw[:, R // 4 : R // 2], w2_scales)
-            elif nm in ("w1w", "w2w"):
-                w = int(nm[1]) - 1
-                nc.sync.dma_start(out=fp4_raw[:, 512 * w : 512 * (w + 1)], in_=(w1_words, w2_words)[w][0].bitcast(I32))
-            elif nm in ("w1a", "w2a", "w1b", "w2b"):
-                w = int(nm[1]) - 1
-                h = "ab".index(nm[2])
-                nc.sync.dma_start(out=fp4_raw[:, 512 * h + 256 * w : 512 * h + 256 * (w + 1)], in_=(w1_words, w2_words)[w][0].bitcast(I32)[:, 256 * h : 256 * (h + 1)])
-            elif nm.startswith("w0"):
-                k = int(nm[2])
-                nc.sync.dma_start(out=tile([P, PACK, 256], F32, "w0r%d" % k), in_=w0_rows[:, :, 256 * k : 256 * (k + 1)])
-            elif nm.startswith("wd"):
-                h = int(nm[2])
-                raw = tile([P, PACK, N], F32, "wdr%d" % h)
-                for e in range(4):
-                    nc.sync.dma_start(out=raw[e:P:4], in_=wd_rows[h, e])
-            else:
-                with nc.allow_non_contiguous_dma(reason="one bias value a partition"):
-                    nc.sync.dma_start(out=bias, in_=b.rearrange("(t p) -> p t", t=PACK))
+        def load_scales(dst, scales):
+            rows = scales[0].bitcast(I32)
+            for quad in (0, 2, 1, 3):
+                nc.sync.dma_start(out=dst[32 * quad : 32 * quad + 4, :], in_=rows[4 * quad : 4 * quad + 4, :])
 
-        def cast(nm, dst, src):
-            e = eng.get(nm, "A")
-            if e == "A":
-                nc.scalar.copy(out=dst, in_=src)
-            elif e == "V":
-                nc.vector.tensor_copy(out=dst, in_=src)
-            else:
-                nc.gpsimd.tensor_copy(out=dst, in_=src)
+        def load_fp4_words(half):
+            for w, words in enumerate((w1_words, w2_words)):
+                src = words[0].bitcast(I32)[:, half * PASS // 2 : (half + 1) * PASS // 2]
+                nc.sync.dma_start(out=fp4_words_raw[:, half, w], in_=src)
+
+        def load_w0(piece):
+            raw = tile([P, PACK, W0_PIECE], F32, "w0_raw%d" % piece)
+            rows = w0.rearrange("(p i) r -> p i r", i=PACK)
+            nc.sync.dma_start(out=raw, in_=rows[:, :, piece * W0_PIECE : (piece + 1) * W0_PIECE])
+            return raw
+
+        def load_wd(half):
+            raw = tile([P, PACK, N], F32, "wd_raw%d" % half)
+            rows = wd.rearrange("(f s t e) n -> f e s t n", f=2, t=PACK, e=RUN)
+            for e in range(RUN):
+                nc.sync.dma_start(out=raw[e:P:RUN], in_=rows[half, e])
+            return raw
+
+        nc.sync.dma_start(offsets[:], offs)
+        load_fp4_words(0)
+        load_scales(table_scales, tab_scales)
+        w0_raw = [load_w0(0)]
+        load_scales(fp4_scales_raw[:, 0], w1_scales)
+        w0_raw.append(load_w0(1))
+        load_scales(fp4_scales_raw[:, 1], w2_scales)
+        nc.sync.dma_start(out=table_words, in_=tab_words[0].rearrange("p t i -> p (t i)").bitcast(I32))
+        w0_raw += [load_w0(2), load_w0(3)]
+        load_fp4_words(1)
+        wd_raw = [load_wd(0), load_wd(1)]
+        with nc.allow_non_contiguous_dma(reason="one bias value for each partition and tile of n"):
+            nc.sync.dma_start(out=bias, in_=b.rearrange("(c p) -> p c", p=P))
+
+        def gather(dst, window, first_j):
+            for g in LIST_ORDER:
+                col = (g * J + first_j) // LIST_GROUP
+                piece = offsets[:, col : col + dst.shape[2] // LIST_GROUP]
+                nc.vector.tensor_copy(dst[:, g, :], window.indirect(piece))
+
+        def gather_words(dst, chunk):
+            gather(dst, table_words.bitcast(U32), chunk * CHUNK)
+
+        def gather_scales(dst, chunk):
+            gather(dst, table_scales.bitcast(U8), chunk * CHUNK)
 
         def quantize(grouped, name):
-            width = grouped.shape[1] // PACK
-            codes = tile([P, width], U32, name + "_codes")
-            planes = tile([P, width], U8, name + "_planes")
-            nc.vector.quantize_mx(out=codes.bitcast(E4M3), scales=planes, in_=grouped)
-            return codes, planes
+            words = tile([P, grouped.shape[1] // PACK], U32, name + "_words")
+            scales = tile([P, grouped.shape[1] // PACK], U8, name + "_scales")
+            nc.vector.quantize_mx(out=words.bitcast(E4M3), scales=scales, in_=grouped)
+            return words, scales
 
-        words_dst = fp4_words.rearrange("p (h w t s e) -> p h w t s e", w=2, h=2, t=PACK, e=2)
-        words_src = fp4_raw.rearrange("p (h w s t e) -> p h w t s e", w=2, h=2, t=PACK, e=2)
-        planes_dst = fp4_planes.rearrange("p (w h t s) -> p h w t s", w=2, h=2, t=PACK)
-        planes_src = fp4_planes_raw.rearrange("p (w h s t) -> p h w t s", w=2, h=2, t=PACK)
-        out_rows = out.rearrange("(t p) j -> p t j", t=PACK)
-        q = {}
-        gw = {j: i for i, g in enumerate(CFG["gw"]) for j in g}
-        gp = {j: i for i, g in enumerate(CFG["gp"]) for j in g}
-        s2 = {j: i for i, g in enumerate(CFG["s2"]) for j in g}
-        for step in CFG["text"]:
-            k = step[0]
-            if k == "G":
-                i = step[1]
-                blocks = CFG["g" + step[2]][i]
-                width = GROUP * len(blocks)
-                for g in (1, 2, 0):
-                    col = (g * J + blocks[0] * GROUP) // 16
-                    piece = offsets[:, col : col + width // 16]
-                    if step[2] == "w":
-                        nc.vector.tensor_copy(tile([P, 3, width], U32, "pw%d" % i)[:, g, :], table.bitcast(U32).indirect(piece))
+        def round_w0(half):
+            grouped = tile([P, PASS * PACK], BF16, "w0_grouped%d" % half)
+            dst = grouped.rearrange("p (t s e i) -> p t s i e", t=PACK, e=RUN, i=PACK)
+            s_piece = W0_PIECE // (PACK * RUN)
+            for n in range(2):
+                src = w0_raw[2 * half + n].rearrange("p i (s t e) -> p t s i e", t=PACK, e=RUN)
+                nc.scalar.copy(out=dst[:, :, n * s_piece : (n + 1) * s_piece], in_=src)
+            return grouped
+
+        def round_wd(half, copies):
+            grouped = tile([P, N * PACK], BF16, "wd_grouped%d" % half)
+            dst = grouped.rearrange("p (c e t) -> p c t e", e=RUN, t=PACK)
+            src = wd_raw[half].rearrange("p t (c e) -> p c t e", e=RUN)
+            for n, copy in enumerate(copies):
+                runs = slice(n * WD_PIECE // RUN, (n + 1) * WD_PIECE // RUN)
+                copy(out=dst[:, runs], in_=src[:, runs])
+            return grouped
+
+        def reorder_fp4_words(half):
+            nc.vector.tensor_copy(
+                out=fp4_words[:, half].rearrange("p w (t s x) -> p w t s x", t=PACK, x=2),
+                in_=fp4_words_raw[:, half].rearrange("p w (s t x) -> p w t s x", t=PACK, x=2),
+            )
+
+        def reorder_fp4_scales():
+            nc.vector.tensor_copy(
+                out=fp4_scales.rearrange("p w f (t s) -> p (w f) t s", t=PACK),
+                in_=fp4_scales_raw.rearrange("p w (f s t) -> p (w f) t s", f=2, t=PACK),
+            )
+
+        def first_layer(chunk, half, h_grouped):
+            sums = [next_bank([P, PACK, BANK_J]) for n in range(CHUNK // BANK_J)]
+            for t in range(PACK):
+                for g in LIST_ORDER:
+                    if g == 0:
+                        lhsT = w0_mx[half][0][:, t * P : (t + 1) * P].bitcast(E4M3)
+                        lhsT_scale = w0_mx[half][1][:, t * P : (t + 1) * P]
                     else:
-                        nc.vector.tensor_copy(tile([P, 3, width], U8, "pp%d" % i)[:, g, :], table_planes.bitcast(U8).indirect(piece))
-            elif k == "C0":
-                n = step[1]
-                grouped = tile([P, PASS * PACK], BF16, "w0g%d" % (n // 2))
-                dst = grouped.rearrange("p (t s e i) -> p t s i e", t=PACK, e=4, i=PACK)
-                src = made["w0r%d" % n].rearrange("p i (s t e) -> p t s i e", t=PACK, e=4)
-                cast("c0%d" % n, dst[:, :, 16 * (n % 2) : 16 * (n % 2) + 16], src)
-            elif k == "Q0":
-                q["w0", step[1]] = quantize(made["w0g%d" % step[1]], "w0q%d" % step[1])
-            elif k == "PW":
-                if not CFG["onep"]:
-                    nc.vector.tensor_copy(out=words_dst[:, step[1]], in_=words_src[:, step[1]])
-                elif step[1] == 0:
-                    nc.vector.tensor_copy(
-                        out=fp4_words.rearrange("p (w t s e) -> p w t s e", w=4, t=PACK, e=2),
-                        in_=fp4_raw.rearrange("p (w s t e) -> p w t s e", w=4, t=PACK, e=2),
-                    )
-            elif k == "PS":
-                nc.vector.tensor_copy(
-                    out=fp4_planes.rearrange("p (w t s) -> p w t s", w=4, t=PACK),
-                    in_=fp4_planes_raw.rearrange("p (w s t) -> p w t s", w=4, t=PACK),
-                )
-            elif k == "CD":
-                n = step[1]
-                grouped = tile([P, PASS * PACK], BF16, "wdg%d" % (n // 2))
-                dst = grouped.rearrange("p (c e t) -> p c t e", e=4, t=PACK)
-                src = made["wdr%d" % (n // 2)].rearrange("p t (c e) -> p c t e", e=4)
-                cols = slice(64 * (n % 2), 64 * (n % 2) + 64)
-                cast("cd%d" % n, dst[:, cols], src[:, cols])
-            elif k == "QD":
-                q["wd", step[1]] = quantize(made["wdg%d" % step[1]], "wdq%d" % step[1])
-            elif k == "F":
-                j0, h = step[1:]
-                if CFG.get("pair"):
-                    js = [] if j0 % 2 else [j0, j0 + 1]
-                else:
-                    js = [j0]
-                accs = [bank("a", [P, PACK, GROUP]) for j in js]
-                for t in range(PACK):
-                    for g in (1, 2, 0):
-                        if g == 0:
-                            lhsT = q["w0", h][0][:, t * P : (t + 1) * P].bitcast(E4M3)
-                            lhsT_scale = q["w0", h][1][:, t * P : (t + 1) * P]
-                        else:
-                            first = (g - 1) * R + h * PASS + t * P
-                            word = (h * R + (g - 1) * PASS + t * P) // 2
-                            lhsT = fp4_words[:, word : word + P // 2].bitcast(E2M1)
-                            lhsT_scale = fp4_planes[:, first // 4 : (first + P) // 4].bitcast(U8)
-                        for j, acc in zip(js, accs):
-                            cw = (j - CFG["gw"][gw[j]][0]) * GROUP
-                            cp = (j - CFG["gp"][gp[j]][0]) * GROUP
-                            nc.tensor.matmul_mx(
-                                out=acc[:, t, :], lhsT=lhsT, lhsT_scale=lhsT_scale,
-                                rhs=made["pw%d" % gw[j]][:, g, cw : cw + GROUP].bitcast(E4M3),
-                                rhs_scale=made["pp%d" % gp[j]][:, g, cp : cp + GROUP], start=(g == 1), stop=(g == 0),
-                            )
-                for j, acc in zip(js, accs):
-                    blocks = CFG["s2"][s2[j]]
-                    grouped = tile([P, len(blocks) * GROUP * PACK], BF16, "hg%d%d" % (s2[j], h))
-                    s = j - blocks[0]
-                    dst = grouped[:, s * GROUP * PACK : (s + 1) * GROUP * PACK].rearrange("p (j t) -> p j t", t=PACK)
-                    if eng.get("r%d%d" % (j, h), "A") == "A":
-                        nc.scalar.activation(dst, acc[:].rearrange("p t j -> p j t"), ACT.Relu)
-                    else:
-                        nc.vector.tensor_scalar_max(dst, acc[:].rearrange("p t j -> p j t"), 0.0)
-            elif k == "W":
-                idle = psum.tile([P, 2, 256], F32, name="bank7")
-                for e in range(step[1]):
-                    nc.tensor.matmul_mx(
-                        out=idle[:, e % 2, :], lhsT=fp4_words[:, 64 * (e % 4) : 64 * (e % 4) + 64].bitcast(E2M1),
-                        lhsT_scale=fp4_planes[:, 32 * (e % 4) : 32 * (e % 4) + 32].bitcast(U8),
-                        rhs=made["pw0"][:, 1, 0:256].bitcast(E4M3), rhs_scale=made["pp0"][:, 1, 0:256], start=True, stop=True,
-                    )
-            elif k == "HQ":
-                i, h = step[1:]
-                q["h", i, h] = quantize(made["hg%d%d" % (i, h)], "hq%d%d" % (i, h))
-            else:
-                i, u = step[1:]
-                blocks = CFG["s2"][i]
-                per = PACK // len(blocks)
-                ts = list(range(u * per, (u + 1) * per))
-                width = GROUP * len(blocks)
-                j0 = blocks[0] * GROUP
-                y = bank("y", [P, per, width])
-                for e, t in enumerate(ts):
-                    for h in range(2):
-                        hq = q["h", i, h]
+                        lhsT = fp4_words[:, half, g - 1, t * P // 2 : (t + 1) * P // 2].bitcast(E2M1)
+                        lhsT_scale = fp4_scales[:, g - 1, half, t * P // 4 : (t + 1) * P // 4].bitcast(U8)
+                    for n, bank in enumerate(sums):
+                        cols = slice(n * BANK_J, (n + 1) * BANK_J)
                         nc.tensor.matmul_mx(
-                            out=y[:, e, :], lhsT=q["wd", h][0][:, t * P : (t + 1) * P].bitcast(E4M3),
-                            lhsT_scale=q["wd", h][1][:, t * P : (t + 1) * P], rhs=hq[0].bitcast(E4M3), rhs_scale=hq[1],
-                            start=(h == 0), stop=(h == 1),
+                            out=bank[:, t, :],
+                            lhsT=lhsT,
+                            lhsT_scale=lhsT_scale,
+                            rhs=picked_words[chunk][:, g, cols].bitcast(E4M3),
+                            rhs_scale=picked_scales[chunk][:, g, cols],
+                            start=(g == LIST_ORDER[0]),
+                            stop=(g == LIST_ORDER[-1]),
                         )
-                result = tile([P, 512], F32, "res%d%d" % (i, u)).rearrange("p (e j) -> p e j", e=per)
-                for e, t in enumerate(ts):
-                    nc.scalar.activation(result[:, e, :], y[:, e, :], ACT.Gelu_apprx_tanh, bias=bias[:, t : t + 1])
-                nc.sync.dma_start(out=out_rows[:, ts[0] : ts[-1] + 1, j0 : j0 + width], in_=result)
+            for n, bank in enumerate(sums):
+                dst = h_grouped[:, n * BANK_J * PACK : (n + 1) * BANK_J * PACK].rearrange("p (j t) -> p j t", t=PACK)
+                src = bank.rearrange("p t j -> p j t")
+                if (chunk * CHUNK // BANK_J + n, half) in RELU_ON_VECTOR:
+                    nc.vector.tensor_scalar_max(dst, src, 0.0)
+                else:
+                    nc.scalar.activation(dst, src, ACT.Relu)
+
+        def chunk_of(h_wide, chunk):
+            first = (chunk * CHUNK % WIDE) * PACK
+            return h_wide[:, first : first + CHUNK * PACK]
+
+        def second_layer(wide, c):
+            y = next_bank([P, WIDE])
+            for half in range(2):
+                nc.tensor.matmul_mx(
+                    out=y,
+                    lhsT=wd_mx[half][0][:, c * P : (c + 1) * P].bitcast(E4M3),
+                    lhsT_scale=wd_mx[half][1][:, c * P : (c + 1) * P],
+                    rhs=h_mx[wide, half][0].bitcast(E4M3),
+                    rhs_scale=h_mx[wide, half][1],
+                    start=(half == 0),
+                    stop=(half == 1),
+                )
+            result = tile([P, WIDE], F32, "result%d_%d" % (wide, c))
+            nc.scalar.activation(result, y, ACT.Gelu_apprx_tanh, bias=bias[:, c : c + 1])
+            nc.sync.dma_start(out=out[c * P : (c + 1) * P, wide * WIDE : (wide + 1) * WIDE], in_=result)
+
+        early_scales = tile([P, 3, 2 * CHUNK], U8, "early_scales")
+        picked_scales = [early_scales[:, :, 0:CHUNK], early_scales[:, :, CHUNK : 2 * CHUNK]]
+        picked_words = [tile([P, 3, CHUNK], U32, "picked_words%d" % chunk) for chunk in range(2)]
+        gather_scales(early_scales, 0)
+        gather_words(picked_words[0], 0)
+        w0_grouped = round_w0(0)
+        reorder_fp4_words(0)
+        reorder_fp4_scales()
+        w0_mx = [quantize(w0_grouped, "w0_mx0")]
+        gather_words(picked_words[1], 1)
+        w0_mx.append(quantize(round_w0(1), "w0_mx1"))
+        reorder_fp4_words(1)
+
+        h_first = tile([P, WIDE * PACK], BF16, "w0_raw3")
+        for chunk in range(2):
+            first_layer(chunk, 0, chunk_of(h_first, chunk))
+
+        late_words = tile([P, 2, 3, CHUNK], U32, "w0_grouped1")
+        late_scales = tile([P, 2, 3, CHUNK], U8, "fp4_words_raw")
+        for n in range(2):
+            picked_words.append(late_words[:, n])
+            picked_scales.append(late_scales[:, n])
+            gather_words(late_words[:, n], 2 + n)
+            gather_scales(late_scales[:, n], 2 + n)
+        h_mx = {(0, 0): quantize(h_first, "h_mx00")}
+        wd_mx = [quantize(round_wd(0, (nc.scalar.copy, nc.vector.tensor_copy)), "wd_mx0")]
+        wd_mx.append(quantize(round_wd(1, (nc.scalar.copy, nc.scalar.copy)), "wd_mx1"))
+
+        h_rest = tile([P, 3, WIDE * PACK], BF16, "wd_raw1")
+        for chunk in range(2):
+            first_layer(chunk, 1, chunk_of(h_rest[:, 0], chunk))
+        h_mx[0, 1] = quantize(h_rest[:, 0], "h_mx01")
+        for half in range(2):
+            first_layer(2, half, chunk_of(h_rest[:, 1 + half], 2))
+        for half in range(2):
+            first_layer(3, half, chunk_of(h_rest[:, 1 + half], 3))
+            h_mx[1, half] = quantize(h_rest[:, 1 + half], "h_mx1%d" % half)
+
+        for wide in range(J // WIDE):
+            for c in range(N // P):
+                second_layer(wide, c)

from contextlib import ExitStack

import concourse.mybir as mybir

K, R, N, T, J = 512, 1024, 512, 2048, 1024
FLOPS = 2 * J * (3 * K * R + R * N)

F32 = mybir.dt.float32
BF16 = mybir.dt.bfloat16
I32 = mybir.dt.int32
U32 = mybir.dt.uint32
U16 = mybir.dt.uint16
U8 = mybir.dt.uint8
E4M3 = mybir.dt.float8_e4m3fn_x4
E2M1 = mybir.dt.float4_e2m1fn_x4
ACT = mybir.ActivationFunctionType

P = 128
PACK = 4
PASS = P * PACK
RUN = 4
LIST_GROUP = 16
BANK_J = 128
CHUNK = 256
WIDE = 512
W0_PIECE = 256
WD_PIECE = 256
BANKS = 8
LIST_ORDER = (1, 2, 0)
RELU_ON_VECTOR = ((7, 0), (7, 1))


def tile_list_rvq_relu_gelu_kernel(
    tc, tab_words, tab_scales, w0, w1_words, w1_scales, w2_words, w2_scales, wd, b, offs, out
):
    nc = tc.nc
    with ExitStack() as ctx:
        sbuf = ctx.enter_context(tc.tile_pool(name="sbuf", bufs=1))
        psum = ctx.enter_context(tc.psum_pool(name="psum", bufs=1))

        def tile(shape, dtype, name):
            return sbuf.tile(shape, dtype, name=name, align_bytes=64)[:]

        banks_taken = []

        def next_bank(shape):
            banks_taken.append(shape)
            return psum.tile(shape, F32, name="bank%d" % ((len(banks_taken) - 1) % BANKS))[:]

        offsets = sbuf.tile([P, 3 * J // LIST_GROUP], U16, name="offsets")
        table_words = tile([P, T], I32, "table_words")
        table_scales = tile([P, T // 4], I32, "table_scales")
        fp4_scales_raw = tile([P, 2, R // 4], I32, "fp4_scales_raw")
        fp4_words_raw = tile([P, 2, 2, PASS // 2], I32, "fp4_words_raw")
        fp4_words = tile([P, 2, 2, PASS // 2], I32, "fp4_words")
        fp4_scales = tile([P, 2, 2, PASS // 4], I32, "fp4_scales")
        bias = tile([P, N // P], F32, "bias")
        warm = tile([P, 2], F32, "warm")

        nc.gpsimd.memset(warm[:, 0:1], 0.0)
        nc.scalar.activation(warm[:, 1:2], warm[:, 0:1], ACT.Gelu_apprx_tanh)

        nc.vector.memset(table_scales, 0)
        nc.vector.memset(fp4_scales_raw.rearrange("p w c -> p (w c)"), 0)

        def load_scales(dst, scales):
            rows = scales[0].bitcast(I32)
            for quad in (0, 2, 1, 3):
                nc.sync.dma_start(out=dst[32 * quad : 32 * quad + 4, :], in_=rows[4 * quad : 4 * quad + 4, :])

        def load_fp4_words(half):
            for w, words in enumerate((w1_words, w2_words)):
                src = words[0].bitcast(I32)[:, half * PASS // 2 : (half + 1) * PASS // 2]
                nc.sync.dma_start(out=fp4_words_raw[:, half, w], in_=src)

        def load_w0(piece):
            raw = tile([P, PACK, W0_PIECE], F32, "w0_raw%d" % piece)
            rows = w0.rearrange("(p i) r -> p i r", i=PACK)
            nc.sync.dma_start(out=raw, in_=rows[:, :, piece * W0_PIECE : (piece + 1) * W0_PIECE])
            return raw

        def load_wd(half):
            raw = tile([P, PACK, N], F32, "wd_raw%d" % half)
            rows = wd.rearrange("(f s t e) n -> f e s t n", f=2, t=PACK, e=RUN)
            for e in range(RUN):
                nc.sync.dma_start(out=raw[e:P:RUN], in_=rows[half, e])
            return raw

        nc.sync.dma_start(offsets[:], offs)
        load_fp4_words(0)
        load_scales(table_scales, tab_scales)
        w0_raw = [load_w0(0)]
        load_scales(fp4_scales_raw[:, 0], w1_scales)
        w0_raw.append(load_w0(1))
        load_scales(fp4_scales_raw[:, 1], w2_scales)
        nc.sync.dma_start(out=table_words, in_=tab_words[0].rearrange("p t i -> p (t i)").bitcast(I32))
        w0_raw += [load_w0(2), load_w0(3)]
        load_fp4_words(1)
        wd_raw = [load_wd(0), load_wd(1)]
        with nc.allow_non_contiguous_dma(reason="one bias value for each partition and tile of n"):
            nc.sync.dma_start(out=bias, in_=b.rearrange("(c p) -> p c", p=P))

        def gather(dst, window, first_j):
            for g in LIST_ORDER:
                col = (g * J + first_j) // LIST_GROUP
                piece = offsets[:, col : col + dst.shape[2] // LIST_GROUP]
                nc.vector.tensor_copy(dst[:, g, :], window.indirect(piece))

        def gather_words(dst, chunk):
            gather(dst, table_words.bitcast(U32), chunk * CHUNK)

        def gather_scales(dst, chunk):
            gather(dst, table_scales.bitcast(U8), chunk * CHUNK)

        def quantize(grouped, name):
            words = tile([P, grouped.shape[1] // PACK], U32, name + "_words")
            scales = tile([P, grouped.shape[1] // PACK], U8, name + "_scales")
            nc.vector.quantize_mx(out=words.bitcast(E4M3), scales=scales, in_=grouped)
            return words, scales

        def round_w0(half):
            grouped = tile([P, PASS * PACK], BF16, "w0_grouped%d" % half)
            dst = grouped.rearrange("p (t s e i) -> p t s i e", t=PACK, e=RUN, i=PACK)
            s_piece = W0_PIECE // (PACK * RUN)
            for n in range(2):
                src = w0_raw[2 * half + n].rearrange("p i (s t e) -> p t s i e", t=PACK, e=RUN)
                nc.scalar.copy(out=dst[:, :, n * s_piece : (n + 1) * s_piece], in_=src)
            return grouped

        def round_wd(half, copies):
            grouped = tile([P, N * PACK], BF16, "wd_grouped%d" % half)
            dst = grouped.rearrange("p (c e t) -> p c t e", e=RUN, t=PACK)
            src = wd_raw[half].rearrange("p t (c e) -> p c t e", e=RUN)
            for n, copy in enumerate(copies):
                runs = slice(n * WD_PIECE // RUN, (n + 1) * WD_PIECE // RUN)
                copy(out=dst[:, runs], in_=src[:, runs])
            return grouped

        def reorder_fp4_words(half):
            nc.vector.tensor_copy(
                out=fp4_words[:, half].rearrange("p w (t s x) -> p w t s x", t=PACK, x=2),
                in_=fp4_words_raw[:, half].rearrange("p w (s t x) -> p w t s x", t=PACK, x=2),
            )

        def reorder_fp4_scales():
            nc.vector.tensor_copy(
                out=fp4_scales.rearrange("p w f (t s) -> p (w f) t s", t=PACK),
                in_=fp4_scales_raw.rearrange("p w (f s t) -> p (w f) t s", f=2, t=PACK),
            )

        def first_layer(chunk, half, h_grouped):
            sums = [next_bank([P, PACK, BANK_J]) for n in range(CHUNK // BANK_J)]
            for t in range(PACK):
                for g in LIST_ORDER:
                    if g == 0:
                        lhsT = w0_mx[half][0][:, t * P : (t + 1) * P].bitcast(E4M3)
                        lhsT_scale = w0_mx[half][1][:, t * P : (t + 1) * P]
                    else:
                        lhsT = fp4_words[:, half, g - 1, t * P // 2 : (t + 1) * P // 2].bitcast(E2M1)
                        lhsT_scale = fp4_scales[:, g - 1, half, t * P // 4 : (t + 1) * P // 4].bitcast(U8)
                    for n, bank in enumerate(sums):
                        cols = slice(n * BANK_J, (n + 1) * BANK_J)
                        nc.tensor.matmul_mx(
                            out=bank[:, t, :],
                            lhsT=lhsT,
                            lhsT_scale=lhsT_scale,
                            rhs=picked_words[chunk][:, g, cols].bitcast(E4M3),
                            rhs_scale=picked_scales[chunk][:, g, cols],
                            start=(g == LIST_ORDER[0]),
                            stop=(g == LIST_ORDER[-1]),
                        )
            for n, bank in enumerate(sums):
                dst = h_grouped[:, n * BANK_J * PACK : (n + 1) * BANK_J * PACK].rearrange("p (j t) -> p j t", t=PACK)
                src = bank.rearrange("p t j -> p j t")
                if (chunk * CHUNK // BANK_J + n, half) in RELU_ON_VECTOR:
                    nc.vector.tensor_scalar_max(dst, src, 0.0)
                else:
                    nc.scalar.activation(dst, src, ACT.Relu)

        def chunk_of(h_wide, chunk):
            first = (chunk * CHUNK % WIDE) * PACK
            return h_wide[:, first : first + CHUNK * PACK]

        def second_layer(wide, c):
            y = next_bank([P, WIDE])
            for half in range(2):
                nc.tensor.matmul_mx(
                    out=y,
                    lhsT=wd_mx[half][0][:, c * P : (c + 1) * P].bitcast(E4M3),
                    lhsT_scale=wd_mx[half][1][:, c * P : (c + 1) * P],
                    rhs=h_mx[wide, half][0].bitcast(E4M3),
                    rhs_scale=h_mx[wide, half][1],
                    start=(half == 0),
                    stop=(half == 1),
                )
            result = tile([P, WIDE], F32, "result%d_%d" % (wide, c))
            nc.scalar.activation(result, y, ACT.Gelu_apprx_tanh, bias=bias[:, c : c + 1])
            nc.sync.dma_start(out=out[c * P : (c + 1) * P, wide * WIDE : (wide + 1) * WIDE], in_=result)

        early_scales = tile([P, 3, 2 * CHUNK], U8, "early_scales")
        picked_scales = [early_scales[:, :, 0:CHUNK], early_scales[:, :, CHUNK : 2 * CHUNK]]
        picked_words = [tile([P, 3, CHUNK], U32, "picked_words%d" % chunk) for chunk in range(2)]
        gather_scales(early_scales, 0)
        gather_words(picked_words[0], 0)
        w0_grouped = round_w0(0)
        reorder_fp4_words(0)
        reorder_fp4_scales()
        w0_mx = [quantize(w0_grouped, "w0_mx0")]
        gather_words(picked_words[1], 1)
        w0_mx.append(quantize(round_w0(1), "w0_mx1"))
        reorder_fp4_words(1)

        h_first = tile([P, WIDE * PACK], BF16, "w0_raw3")
        for chunk in range(2):
            first_layer(chunk, 0, chunk_of(h_first, chunk))

        late_words = tile([P, 2, 3, CHUNK], U32, "w0_grouped1")
        late_scales = tile([P, 2, 3, CHUNK], U8, "fp4_words_raw")
        for n in range(2):
            picked_words.append(late_words[:, n])
            picked_scales.append(late_scales[:, n])
            gather_words(late_words[:, n], 2 + n)
            gather_scales(late_scales[:, n], 2 + n)
        h_mx = {(0, 0): quantize(h_first, "h_mx00")}
        wd_mx = [quantize(round_wd(0, (nc.scalar.copy, nc.vector.tensor_copy)), "wd_mx0")]
        wd_mx.append(quantize(round_wd(1, (nc.scalar.copy, nc.scalar.copy)), "wd_mx1"))

        h_rest = tile([P, 3, WIDE * PACK], BF16, "wd_raw1")
        for chunk in range(2):
            first_layer(chunk, 1, chunk_of(h_rest[:, 0], chunk))
        h_mx[0, 1] = quantize(h_rest[:, 0], "h_mx01")
        for half in range(2):
            first_layer(2, half, chunk_of(h_rest[:, 1 + half], 2))
        for half in range(2):
            first_layer(3, half, chunk_of(h_rest[:, 1 + half], 3))
            h_mx[1, half] = quantize(h_rest[:, 1 + half], "h_mx1%d" % half)

        for wide in range(J // WIDE):
            for c in range(N // P):
                second_layer(wide, c)
